import numpy as np
import ml_dtypes


def mxq(x, axis, fmt="e4m3"):
    dtype, down = {"e4m3": (ml_dtypes.float8_e4m3fn, 7), "e5m2": (ml_dtypes.float8_e5m2, 14)}[fmt]
    v = np.moveaxis(np.asarray(x, np.float32).astype(ml_dtypes.bfloat16).astype(np.float64), axis, -1)
    blocks = v.reshape(v.shape[:-1] + (-1, 32))
    amax = np.abs(blocks).max(-1, keepdims=True)
    byte = np.maximum(np.where(amax > 0, np.frexp(amax)[1] - 1 + 127, 0) - down, 1)
    scale = np.exp2(byte - 127.0)
    codes = (blocks / scale).astype(np.float32).astype(dtype).astype(np.float64)
    return np.moveaxis((codes * scale).reshape(v.shape), -1, axis)


WIDE = False


def mx_kscale(k):
    if not WIDE:
        return np.ones(k)
    levels = np.array([10, -10, 5, -5, 0])
    if k % 512:
        return np.exp2(np.random.permutation(np.resize(levels, k // 32))).repeat(32)
    a = np.empty((k // 512, 16))
    for p in range(k // 512):
        a[p, :8] = np.random.permutation(np.resize(levels, 8))
        for g in range(8):
            far = levels[np.abs(levels - a[p, g]) >= 10]
            a[p, g + 8] = far[np.random.randint(len(far))]
    return np.exp2(a.ravel()).repeat(32)


def f64(x):
    return np.asarray(x).astype(np.float64)


E2M1 = np.array([0.0, 0.5, 1.0, 1.5, 2.0, 3.0, 4.0, 6.0, -0.0, -0.5, -1.0, -1.5, -2.0, -3.0, -4.0, -6.0])


def pack_weight(w, fmt):
    k, n = w.shape
    w = f64(np.asarray(w, np.float32).astype(ml_dtypes.bfloat16)).reshape(k // 32, 32, n)
    amax = np.abs(w).max(1)
    if fmt == "e4m3":
        byte = np.frexp(amax)[1] - 1 + 127 - 7
    else:
        mant, ex = np.frexp(amax / 6.0)
        byte = np.where(mant > 0.5, ex, ex - 1) + 127
    byte = np.clip(np.where(amax > 0, byte, 1), 1, 254)
    scaled = (w * np.exp2(127.0 - byte)[:, None, :]).reshape(k, n).astype(np.float32)
    by_word = np.ascontiguousarray(scaled.reshape(k // 512, 128, 4, n).transpose(0, 1, 3, 2))
    if fmt == "e4m3":
        words = by_word.astype(ml_dtypes.float8_e4m3fn).view(np.uint8)
    else:
        c = by_word.astype(ml_dtypes.float4_e2m1fn).view(np.uint8) & 0xF
        words = (c[..., 0::2] | (c[..., 1::2] << 4)).reshape(k // 512, 128, 2 * n)
    return np.ascontiguousarray(words), np.ascontiguousarray(byte.astype(np.uint8).reshape(k // 512, 16, n))


def unpack_weight(words, scales, fmt):
    g, _, n = scales.shape
    words = np.ascontiguousarray(words).reshape(g, 128, n, -1)
    if fmt == "e4m3":
        vals = words.view(ml_dtypes.float8_e4m3fn).astype(np.float64)
    else:
        nib = np.empty((g, 128, n, 4), np.uint8)
        nib[..., 0::2] = words & 0xF
        nib[..., 1::2] = words >> 4
        vals = E2M1[nib]
    vals = vals * np.repeat(np.exp2(scales.astype(np.float64) - 127.0), 8, axis=1)[..., None]
    return vals.transpose(0, 1, 3, 2).reshape(g * 512, n)


def planes(y):
    n, m = y.shape
    v = y.astype(np.float32).astype(ml_dtypes.bfloat16).astype(np.float64).reshape(n // 32, 32, m)
    top = np.abs(v).max(1)
    byte = np.clip(np.where(top > 0, np.frexp(top)[1] - 1 + 127 - 7, 1), 1, 254)
    codes = (v * np.exp2(127.0 - byte)[:, None, :]).reshape(n, m).astype(np.float32).astype(ml_dtypes.float8_e4m3fn).view(np.uint8)
    words = codes.reshape(n // 512, 128, 4, m).transpose(0, 1, 3, 2)
    return np.ascontiguousarray(words), np.ascontiguousarray(byte.astype(np.uint8).reshape(n // 512, 16, m))


K, M, T = 512, 512, 1024


def setup_inputs():
    n = np.random.standard_normal
    s = mx_kscale(K)[:, None]
    u = mx_kscale(T)[:, None]
    q = n((K, T)) * s
    p_vc = pack_weight(0.1 * n((T, M)) / u, "e2m1")
    return {
        "qc": (q).astype(np.float32),
        "kc": (n((K, T)) / np.sqrt(K) / s).astype(np.float32),
        "qd": (q * 0.995 ** (np.arange(T) + 1.0)).astype(np.float32),
        "st": (n((K, M)) / np.sqrt(K) / s).astype(np.float32),
        "vc_words": p_vc[0],
        "vc_scales": p_vc[1],
        "dm": (np.tril(0.995 ** (np.arange(T)[:, None] - np.arange(T)[None])).T * u).astype(np.float32),
        "g": (n((1024, 512))).astype(np.float32),
    }


def reference(qc, kc, qd, st, vc_words, vc_scales, dm, g):
    qc_ = mxq(f64(qc), 0, "e4m3")
    kc_ = mxq(f64(kc), 0, "e4m3")
    qd_ = mxq(f64(qd), 0, "e4m3")
    st_ = mxq(f64(st), 0, "e4m3")
    vc_ = unpack_weight(vc_words, vc_scales, "e2m1")
    h_ = mxq((kc_.T @ qc_) * f64(dm), 0, "e4m3")
    y = h_.T @ vc_ + qd_.T @ st_
    out_0 = f64(g) * y
    return (out_0,) + planes(out_0)

@@ -1,0 +1,213 @@
+from contextlib import ExitStack
+
+import concourse.mybir as mybir
+
+K, M, T = 512, 512, 1024
+FLOPS = 2 * K * T * T + 2 * T * T * M + 2 * K * T * M
+
+F32 = mybir.dt.float32
+BF16 = mybir.dt.bfloat16
+I32 = mybir.dt.int32
+U32 = mybir.dt.uint32
+U8 = mybir.dt.uint8
+FP8X4 = mybir.dt.float8_e4m3fn_x4
+FP4X4 = mybir.dt.float4_e2m1fn_x4
+MULT = mybir.AluOpType.mult
+
+P = 128
+PACK = 4
+HALF = P * PACK
+CHUNK = 128
+RUN = 4
+QUADS = 4
+ST_SPLIT = 256
+OUT_SPLIT = 320
+
+
+def tile_mix_linattn_tm_pl_mul_kernel(tc, qc, kc, qd, st, vc_words, vc_scales, dm, g, out_0, out_1, out_2):
+    nc = tc.nc
+
+    with ExitStack() as ctx:
+        sb = ctx.enter_context(tc.tile_pool(name="sb", bufs=1))
+        ps = ctx.enter_context(tc.psum_pool(name="ps", bufs=1))
+        ctx.enter_context(tc.manual_schedule())
+
+        def half(a):
+            return slice(a * HALF, (a + 1) * HALF)
+
+        def load(name, rows):
+            raw = sb.tile([P, PACK, rows.shape[1]], F32, name=name, align_bytes=64)
+            nc.sync.dma_start(out=raw[:], in_=rows.rearrange("(p i) w -> p i w", i=PACK))
+            return raw
+
+        def new_operand(name):
+            grouped = sb.tile([P, HALF * PACK], BF16, name=name + "_bf", align_bytes=64)
+            codes = sb.tile([P, HALF], U32, name=name + "_codes", align_bytes=64)
+            scales = sb.tile([P, HALF], U8, name=name + "_scales", align_bytes=64)
+            return grouped, codes, scales
+
+        def copy_on(engine, dst, src):
+            if engine == "vector":
+                nc.vector.tensor_copy(out=dst, in_=src)
+            else:
+                nc.scalar.copy(out=dst, in_=src)
+
+        def round_plain(engine, grouped, raw, c0, c1):
+            dst = grouped[:, c0 * PACK : c1 * PACK].rearrange("p (c w i) -> p c i w", w=RUN, i=PACK)
+            copy_on(engine, dst, raw[:, :, c0:c1].rearrange("p i (c w) -> p c i w", w=RUN))
+
+        def round_dealt(engine, grouped, raw):
+            dst = grouped[:].rearrange("p (r m i) -> p m i r", r=PACK, i=PACK)
+            copy_on(engine, dst, raw.rearrange("p i (m r) -> p m i r", r=PACK))
+
+        def quantize(grouped, codes, scales):
+            nc.vector.quantize_mx(out=codes.bitcast(FP8X4), scales=scales, in_=grouped)
+
+        def quantize_operand(op):
+            quantize(op[0][:], op[1][:], op[2][:])
+
+        def scores(first_bank, keys, queries):
+            banks = []
+            for c in range(HALF // CHUNK):
+                bank = ps.tile([P, PACK, CHUNK], F32, name="bank%d" % (first_bank + c))
+                cols = slice(c * CHUNK, (c + 1) * CHUNK)
+                for i in range(PACK):
+                    rows = slice(i * P, (i + 1) * P)
+                    nc.tensor.matmul_mx(
+                        out=bank[:, i, :],
+                        lhsT=keys[1][:, rows].bitcast(FP8X4),
+                        lhsT_scale=keys[2][:, rows],
+                        rhs=queries[1][:, cols].bitcast(FP8X4),
+                        rhs_scale=queries[2][:, cols],
+                        start=True,
+                        stop=True,
+                    )
+                banks.append(bank)
+            return banks
+
+        def decay(h, banks, dm_block, c):
+            m_cols = CHUNK // PACK
+            dst = h[0][:].rearrange("p (r m i) -> p m i r", r=PACK, i=PACK)[:, c * m_cols : (c + 1) * m_cols, :, :]
+            nc.vector.tensor_tensor(
+                out=dst,
+                in0=banks[c][:].rearrange("p i (m r) -> p m i r", r=PACK),
+                in1=dm_block[:, :, c * CHUNK : (c + 1) * CHUNK].rearrange("p i (m r) -> p m i r", r=PACK),
+                op=MULT,
+            )
+
+        def y_pass(banks, stationary, moving_codes, moving_scales, start, stop):
+            for r in range(PACK):
+                cols = slice(r * P, (r + 1) * P)
+                nc.tensor.matmul_mx(
+                    out=banks[r][:],
+                    lhsT=stationary[1][:, cols].bitcast(FP8X4),
+                    lhsT_scale=stationary[2][:, cols],
+                    rhs=moving_codes,
+                    rhs_scale=moving_scales,
+                    start=start,
+                    stop=stop,
+                )
+
+        def y_banks(first_bank):
+            banks = []
+            for r in range(PACK):
+                bank = ps.tile([P, M], F32, name="bank%d" % (first_bank + r))
+                banks.append(bank)
+            return banks
+
+        def gate(result, banks, g_raw, r):
+            nc.vector.tensor_tensor(out=result[:, r, :], in0=banks[r][:], in1=g_raw[:, r, :], op=MULT)
+
+        def store_rows(result, a, r0, r1):
+            rows = out_0[half(a), :].rearrange("(p r) n -> p r n", r=PACK)
+            nc.sync.dma_start(out=rows[:, r0:r1, :], in_=result[:, r0:r1, :])
+
+        vc_plane = sb.tile([P, 2, M], U8, name="vc_plane", align_bytes=64)
+        nc.vector.memset(vc_plane[:].rearrange("p a n -> p (a n)").bitcast(U32), 0)
+        for q in range(QUADS):
+            nc.scalar.dma_start(
+                out=vc_plane[32 * q : 32 * q + 4, :, :].bitcast(I32),
+                in_=vc_scales[:, 4 * q : 4 * q + 4, :].rearrange("a q n -> q a n").bitcast(I32),
+            )
+
+        kc0_raw = load("kc0_raw", kc[:, half(0)])
+        qc_raw = load("qc_raw", qc)
+        dm0_raw = load("dm0_raw", dm[half(0), :])
+        kc1_raw = load("kc1_raw", kc[:, half(1)])
+        vc_codes = sb.tile([P, 2, 2 * M], U8, name="vc_codes", align_bytes=64)
+        nc.sync.dma_start(out=vc_codes[:].bitcast(I32), in_=vc_words.rearrange("a p b -> p a b").bitcast(I32))
+        dm11_raw = load("dm11_raw", dm[half(1), half(1)])
+        qd_raw = load("qd_raw", qd)
+        st_raw = load("st_raw", st)
+        g_raw = [load("g%d_raw" % a, g[half(a), :]) for a in range(2)]
+
+        kc_op = [new_operand("kc%d" % a) for a in range(2)]
+        qc_op = [new_operand("qc%d" % a) for a in range(2)]
+        qd_op = [new_operand("qd%d" % a) for a in range(2)]
+        st_op = new_operand("st")
+        h00, h01, h11 = new_operand("h00"), new_operand("h01"), new_operand("h11")
+        vc_op = [(vc_codes[:, a, :].bitcast(FP4X4), vc_plane[:, a, :]) for a in range(2)]
+
+        round_dealt("vector", kc_op[0][0], kc0_raw[:])
+        quantize_operand(kc_op[0])
+        round_plain("vector", qc_op[0][0], qc_raw[:, :, half(0)], 0, HALF)
+        round_plain("scalar", qc_op[1][0], qc_raw[:, :, half(1)], 0, HALF)
+        quantize_operand(qc_op[0])
+        s00 = scores(0, kc_op[0], qc_op[0])
+        quantize_operand(qc_op[1])
+        s01 = scores(4, kc_op[0], qc_op[1])
+        round_dealt("scalar", kc_op[1][0], kc1_raw[:])
+
+        dm00, dm01 = dm0_raw[:, :, half(0)], dm0_raw[:, :, half(1)]
+        for c in range(4):
+            decay(h00, s00, dm00, c)
+        decay(h01, s01, dm01, 0)
+        quantize_operand(h00)
+        decay(h01, s01, dm01, 1)
+        decay(h01, s01, dm01, 2)
+        quantize_operand(kc_op[1])
+        s11 = scores(0, kc_op[1], qc_op[1])
+        decay(h01, s01, dm01, 3)
+        y0 = y_banks(4)
+        y_pass(y0, h00, vc_op[0][0], vc_op[0][1], True, False)
+        decay(h11, s11, dm11_raw[:], 0)
+        quantize_operand(h01)
+        for c in range(1, 4):
+            decay(h11, s11, dm11_raw[:], c)
+        y1 = y_banks(0)
+        y_pass(y1, h01, vc_op[0][0], vc_op[0][1], True, False)
+
+        round_dealt("scalar", qd_op[0][0], qd_raw[:, :, half(0)])
+        round_dealt("vector", qd_op[1][0], qd_raw[:, :, half(1)])
+        quantize_operand(h11)
+        y_pass(y1, h11, vc_op[1][0], vc_op[1][1], False, False)
+        quantize_operand(qd_op[1])
+        round_plain("vector", st_op[0], st_raw[:], 0, ST_SPLIT)
+        round_plain("scalar", st_op[0], st_raw[:], ST_SPLIT, M)
+        quantize_operand(qd_op[0])
+        quantize_operand(st_op)
+        y_pass(y0, qd_op[0], st_op[1][:].bitcast(FP8X4), st_op[2][:], False, True)
+        y_pass(y1, qd_op[1], st_op[1][:].bitcast(FP8X4), st_op[2][:], False, True)
+
+        result = [sb.tile([P, PACK, M], F32, name="result%d" % a, align_bytes=64) for a in range(2)]
+        out_bf = [sb.tile([P, M * PACK], BF16, name="out_bf%d" % a, align_bytes=64) for a in range(2)]
+        out_codes = [sb.tile([P, M], U32, name="out_codes%d" % a, align_bytes=64) for a in range(2)]
+        out_plane = sb.tile([P, 2, M], U8, name="out_plane", align_bytes=64)
+        for a, banks in enumerate((y0, y1)):
+            for r in range(PACK):
+                gate(result[a], banks, g_raw[a], r)
+                if r % 2 == 1:
+                    store_rows(result[a], a, r - 1, r + 1)
+            if a == 0:
+                round_plain("scalar", out_bf[0], result[0][:], 0, M)
+        round_plain("vector", out_bf[1], result[1][:], 0, OUT_SPLIT)
+        round_plain("scalar", out_bf[1], result[1][:], OUT_SPLIT, M)
+        for a in range(2):
+            quantize(out_bf[a][:], out_codes[a][:], out_plane[:, a, :])
+            nc.sync.dma_start(out=out_1[a].rearrange("p n i -> p (n i)").bitcast(I32), in_=out_codes[a][:].bitcast(I32))
+        for q in range(QUADS):
+            engine = nc.sync if q % 2 == 0 else nc.scalar
+            engine.dma_start(
+                out=out_2[:, 4 * q : 4 * q + 4, :].rearrange("a q n -> q a n").bitcast(I32),
+                in_=out_plane[32 * q : 32 * q + 4, :, :].bitcast(I32),
+            )

@@ -20,8 +20,7 @@ HALF = P * PACK
 CHUNK = 128
 RUN = 4
 QUADS = 4
-ST_SPLIT = 256
-OUT_SPLIT = 320
+PLAIN_SPLIT = 384
 
 
 def tile_mix_linattn_tm_pl_mul_kernel(tc, qc, kc, qd, st, vc_words, vc_scales, dm, g, out_0, out_1, out_2):
@@ -56,9 +55,25 @@ def tile_mix_linattn_tm_pl_mul_kernel(tc, qc, kc, qd, st, vc_words, vc_scales, d
             dst = grouped[:, c0 * PACK : c1 * PACK].rearrange("p (c w i) -> p c i w", w=RUN, i=PACK)
             copy_on(engine, dst, raw[:, :, c0:c1].rearrange("p i (c w) -> p c i w", w=RUN))
 
-        def round_dealt(engine, grouped, raw):
-            dst = grouped[:].rearrange("p (r m i) -> p m i r", r=PACK, i=PACK)
-            copy_on(engine, dst, raw.rearrange("p i (m r) -> p m i r", r=PACK))
+        def round_dealt(engine, grouped, raw, m0, m1, raw_m0=0):
+            dst = grouped[:].rearrange("p (r m i) -> p m i r", r=PACK, i=PACK)[:, m0:m1, :, :]
+            src = raw[:, :, (m0 - raw_m0) * PACK : (m1 - raw_m0) * PACK]
+            copy_on(engine, dst, src.rearrange("p i (m r) -> p m i r", r=PACK))
+
+        def shared_plain(grouped, raw):
+            round_plain("vector", grouped, raw, 0, PLAIN_SPLIT)
+            round_plain("scalar", grouped, raw, PLAIN_SPLIT, HALF)
+
+        def shared_dealt(grouped, raw, m0, m1, split, raw_m0=0):
+            round_dealt("vector", grouped, raw, m0, split, raw_m0)
+            round_dealt("scalar", grouped, raw, split, m1, raw_m0)
+
+        def load_gate(a):
+            raw = sb.tile([P, PACK, M], F32, name="g%d_raw" % a, align_bytes=64)
+            rows = g[half(a), :].rearrange("(p r) n -> p r n", r=PACK)
+            for r0 in (0, 2):
+                nc.sync.dma_start(out=raw[:, r0 : r0 + 2, :], in_=rows[:, r0 : r0 + 2, :])
+            return raw
 
         def quantize(grouped, codes, scales):
             nc.vector.quantize_mx(out=codes.bitcast(FP8X4), scales=scales, in_=grouped)
@@ -130,16 +145,17 @@ def tile_mix_linattn_tm_pl_mul_kernel(tc, qc, kc, qd, st, vc_words, vc_scales, d
                 in_=vc_scales[:, 4 * q : 4 * q + 4, :].rearrange("a q n -> q a n").bitcast(I32),
             )
 
-        kc0_raw = load("kc0_raw", kc[:, half(0)])
+        kc_raw = load("kc_raw", kc)
         qc_raw = load("qc_raw", qc)
         dm0_raw = load("dm0_raw", dm[half(0), :])
-        kc1_raw = load("kc1_raw", kc[:, half(1)])
+        st_raw = load("st_raw", st)
+        qd0_raw = load("qd0_raw", qd[:, half(0)])
         vc_codes = sb.tile([P, 2, 2 * M], U8, name="vc_codes", align_bytes=64)
         nc.sync.dma_start(out=vc_codes[:].bitcast(I32), in_=vc_words.rearrange("a p b -> p a b").bitcast(I32))
-        dm11_raw = load("dm11_raw", dm[half(1), half(1)])
-        qd_raw = load("qd_raw", qd)
-        st_raw = load("st_raw", st)
-        g_raw = [load("g%d_raw" % a, g[half(a), :]) for a in range(2)]
+        dm11 = load("dm11_raw", dm[half(1), half(1)])
+        qd1_raw = load("qd1_raw", qd[:, half(1)])
+        g0_raw = load_gate(0)
+        g1_raw = load_gate(1)
 
         kc_op = [new_operand("kc%d" % a) for a in range(2)]
         qc_op = [new_operand("qc%d" % a) for a in range(2)]
@@ -147,64 +163,67 @@ def tile_mix_linattn_tm_pl_mul_kernel(tc, qc, kc, qd, st, vc_words, vc_scales, d
         st_op = new_operand("st")
         h00, h01, h11 = new_operand("h00"), new_operand("h01"), new_operand("h11")
         vc_op = [(vc_codes[:, a, :].bitcast(FP4X4), vc_plane[:, a, :]) for a in range(2)]
+        result = [sb.tile([P, PACK, M], F32, name="result%d" % a, align_bytes=64) for a in range(2)]
+        out_bf = [sb.tile([P, M * PACK], BF16, name="out_bf%d" % a, align_bytes=64) for a in range(2)]
+        out_codes = [sb.tile([P, M], U32, name="out_codes%d" % a, align_bytes=64) for a in range(2)]
+        out_plane = sb.tile([P, 2, M], U8, name="out_plane", align_bytes=64)
 
-        round_dealt("vector", kc_op[0][0], kc0_raw[:])
+        def out_planes(a):
+            quantize(out_bf[a][:], out_codes[a][:], out_plane[:, a, :])
+            nc.sync.dma_start(out=out_1[a].rearrange("p n i -> p (n i)").bitcast(I32), in_=out_codes[a][:].bitcast(I32))
+
+        dm00, dm01 = dm0_raw[:, :, half(0)], dm0_raw[:, :, half(1)]
+        st_codes, st_scales = st_op[1][:].bitcast(FP8X4), st_op[2][:]
+        round_dealt("vector", kc_op[0][0], kc_raw[:, :, half(0)], 0, P)
+        round_dealt("scalar", kc_op[1][0], kc_raw[:, :, half(1)], 0, P)
         quantize_operand(kc_op[0])
+        quantize_operand(kc_op[1])
         round_plain("vector", qc_op[0][0], qc_raw[:, :, half(0)], 0, HALF)
         round_plain("scalar", qc_op[1][0], qc_raw[:, :, half(1)], 0, HALF)
         quantize_operand(qc_op[0])
         s00 = scores(0, kc_op[0], qc_op[0])
         quantize_operand(qc_op[1])
         s01 = scores(4, kc_op[0], qc_op[1])
-        round_dealt("scalar", kc_op[1][0], kc1_raw[:])
-
-        dm00, dm01 = dm0_raw[:, :, half(0)], dm0_raw[:, :, half(1)]
+        round_plain("scalar", st_op[0], st_raw[:], 0, M)
+        round_dealt("scalar", qd_op[0][0], qd0_raw[:], 0, P)
         for c in range(4):
             decay(h00, s00, dm00, c)
+        s11 = scores(0, kc_op[1], qc_op[1])
         decay(h01, s01, dm01, 0)
         quantize_operand(h00)
-        decay(h01, s01, dm01, 1)
-        decay(h01, s01, dm01, 2)
-        quantize_operand(kc_op[1])
-        s11 = scores(0, kc_op[1], qc_op[1])
-        decay(h01, s01, dm01, 3)
+        for c in range(1, 4):
+            decay(h01, s01, dm01, c)
         y0 = y_banks(4)
         y_pass(y0, h00, vc_op[0][0], vc_op[0][1], True, False)
-        decay(h11, s11, dm11_raw[:], 0)
+        quantize_operand(st_op)
         quantize_operand(h01)
-        for c in range(1, 4):
-            decay(h11, s11, dm11_raw[:], c)
+        quantize_operand(qd_op[0])
+        y_pass(y0, qd_op[0], st_codes, st_scales, False, True)
+        for c in range(4):
+            decay(h11, s11, dm11[:], c)
         y1 = y_banks(0)
         y_pass(y1, h01, vc_op[0][0], vc_op[0][1], True, False)
-
-        round_dealt("scalar", qd_op[0][0], qd_raw[:, :, half(0)])
-        round_dealt("vector", qd_op[1][0], qd_raw[:, :, half(1)])
+        shared_dealt(qd_op[1][0], qd1_raw[:], 0, P, 32)
         quantize_operand(h11)
         y_pass(y1, h11, vc_op[1][0], vc_op[1][1], False, False)
+        gate(result[0], y0, g0_raw, 0)
+        gate(result[0], y0, g0_raw, 1)
+        store_rows(result[0], 0, 0, 2)
         quantize_operand(qd_op[1])
-        round_plain("vector", st_op[0], st_raw[:], 0, ST_SPLIT)
-        round_plain("scalar", st_op[0], st_raw[:], ST_SPLIT, M)
-        quantize_operand(qd_op[0])
-        quantize_operand(st_op)
-        y_pass(y0, qd_op[0], st_op[1][:].bitcast(FP8X4), st_op[2][:], False, True)
-        y_pass(y1, qd_op[1], st_op[1][:].bitcast(FP8X4), st_op[2][:], False, True)
-
-        result = [sb.tile([P, PACK, M], F32, name="result%d" % a, align_bytes=64) for a in range(2)]
-        out_bf = [sb.tile([P, M * PACK], BF16, name="out_bf%d" % a, align_bytes=64) for a in range(2)]
-        out_codes = [sb.tile([P, M], U32, name="out_codes%d" % a, align_bytes=64) for a in range(2)]
-        out_plane = sb.tile([P, 2, M], U8, name="out_plane", align_bytes=64)
-        for a, banks in enumerate((y0, y1)):
-            for r in range(PACK):
-                gate(result[a], banks, g_raw[a], r)
-                if r % 2 == 1:
-                    store_rows(result[a], a, r - 1, r + 1)
-            if a == 0:
-                round_plain("scalar", out_bf[0], result[0][:], 0, M)
-        round_plain("vector", out_bf[1], result[1][:], 0, OUT_SPLIT)
-        round_plain("scalar", out_bf[1], result[1][:], OUT_SPLIT, M)
-        for a in range(2):
-            quantize(out_bf[a][:], out_codes[a][:], out_plane[:, a, :])
-            nc.sync.dma_start(out=out_1[a].rearrange("p n i -> p (n i)").bitcast(I32), in_=out_codes[a][:].bitcast(I32))
+        y_pass(y1, qd_op[1], st_codes, st_scales, False, True)
+        gate(result[0], y0, g0_raw, 2)
+        gate(result[0], y0, g0_raw, 3)
+        store_rows(result[0], 0, 2, 4)
+        round_plain("scalar", out_bf[0], result[0][:], 0, M)
+        gate(result[1], y1, g1_raw, 0)
+        gate(result[1], y1, g1_raw, 1)
+        store_rows(result[1], 1, 0, 2)
+        gate(result[1], y1, g1_raw, 2)
+        gate(result[1], y1, g1_raw, 3)
+        store_rows(result[1], 1, 2, 4)
+        shared_plain(out_bf[1], result[1][:])
+        out_planes(0)
+        out_planes(1)
         for q in range(QUADS):
             engine = nc.sync if q % 2 == 0 else nc.scalar
             engine.dma_start(

@@ -56,9 +56,9 @@ def tile_mix_linattn_tm_pl_mul_kernel(tc, qc, kc, qd, st, vc_words, vc_scales, d
             copy_on(engine, dst, raw[:, :, c0:c1].rearrange("p i (c w) -> p c i w", w=RUN))
 
         def round_dealt(engine, grouped, raw, m0, m1, raw_m0=0):
-            dst = grouped[:].rearrange("p (r m i) -> p m i r", r=PACK, i=PACK)[:, m0:m1, :, :]
+            dst = grouped[:].rearrange("p (r m i) -> p m r i", r=PACK, i=PACK)[:, m0:m1, :, :]
             src = raw[:, :, (m0 - raw_m0) * PACK : (m1 - raw_m0) * PACK]
-            copy_on(engine, dst, src.rearrange("p i (m r) -> p m i r", r=PACK))
+            copy_on(engine, dst, src.rearrange("p i (m r) -> p m r i", r=PACK))
 
         def shared_plain(grouped, raw):
             round_plain("vector", grouped, raw, 0, PLAIN_SPLIT)
@@ -102,11 +102,11 @@ def tile_mix_linattn_tm_pl_mul_kernel(tc, qc, kc, qd, st, vc_words, vc_scales, d
 
         def decay(h, banks, dm_block, c):
             m_cols = CHUNK // PACK
-            dst = h[0][:].rearrange("p (r m i) -> p m i r", r=PACK, i=PACK)[:, c * m_cols : (c + 1) * m_cols, :, :]
+            dst = h[0][:].rearrange("p (r m i) -> p m r i", r=PACK, i=PACK)[:, c * m_cols : (c + 1) * m_cols, :, :]
             nc.vector.tensor_tensor(
                 out=dst,
-                in0=banks[c][:].rearrange("p i (m r) -> p m i r", r=PACK),
-                in1=dm_block[:, :, c * CHUNK : (c + 1) * CHUNK].rearrange("p i (m r) -> p m i r", r=PACK),
+                in0=banks[c][:].rearrange("p i (m r) -> p m r i", r=PACK),
+                in1=dm_block[:, :, c * CHUNK : (c + 1) * CHUNK].rearrange("p i (m r) -> p m r i", r=PACK),
                 op=MULT,
             )
 
@@ -214,14 +214,16 @@ def tile_mix_linattn_tm_pl_mul_kernel(tc, qc, kc, qd, st, vc_words, vc_scales, d
         gate(result[0], y0, g0_raw, 2)
         gate(result[0], y0, g0_raw, 3)
         store_rows(result[0], 0, 2, 4)
-        round_plain("scalar", out_bf[0], result[0][:], 0, M)
+        round_plain("scalar", out_bf[0], result[0][:], 96, M)
         gate(result[1], y1, g1_raw, 0)
         gate(result[1], y1, g1_raw, 1)
         store_rows(result[1], 1, 0, 2)
         gate(result[1], y1, g1_raw, 2)
         gate(result[1], y1, g1_raw, 3)
         store_rows(result[1], 1, 2, 4)
-        shared_plain(out_bf[1], result[1][:])
+        round_plain("vector", out_bf[0], result[0][:], 0, 96)
+        round_plain("scalar", out_bf[1], result[1][:], 288, M)
+        round_plain("vector", out_bf[1], result[1][:], 0, 288)
         out_planes(0)
         out_planes(1)
         for q in range(QUADS):

from contextlib import ExitStack

import concourse.mybir as mybir

K, M, T = 512, 512, 1024
FLOPS = 2 * K * T * T + 2 * T * T * M + 2 * K * T * M

F32 = mybir.dt.float32
BF16 = mybir.dt.bfloat16
I32 = mybir.dt.int32
U32 = mybir.dt.uint32
U8 = mybir.dt.uint8
FP8X4 = mybir.dt.float8_e4m3fn_x4
FP4X4 = mybir.dt.float4_e2m1fn_x4
MULT = mybir.AluOpType.mult

P = 128
PACK = 4
HALF = P * PACK
CHUNK = 128
RUN = 4
QUADS = 4
PLAIN_SPLIT = 384


def tile_mix_linattn_tm_pl_mul_kernel(tc, qc, kc, qd, st, vc_words, vc_scales, dm, g, out_0, out_1, out_2):
    nc = tc.nc

    with ExitStack() as ctx:
        sb = ctx.enter_context(tc.tile_pool(name="sb", bufs=1))
        ps = ctx.enter_context(tc.psum_pool(name="ps", bufs=1))
        ctx.enter_context(tc.manual_schedule())

        def half(a):
            return slice(a * HALF, (a + 1) * HALF)

        def load(name, rows):
            raw = sb.tile([P, PACK, rows.shape[1]], F32, name=name, align_bytes=64)
            nc.sync.dma_start(out=raw[:], in_=rows.rearrange("(p i) w -> p i w", i=PACK))
            return raw

        def new_operand(name):
            grouped = sb.tile([P, HALF * PACK], BF16, name=name + "_bf", align_bytes=64)
            codes = sb.tile([P, HALF], U32, name=name + "_codes", align_bytes=64)
            scales = sb.tile([P, HALF], U8, name=name + "_scales", align_bytes=64)
            return grouped, codes, scales

        def copy_on(engine, dst, src):
            if engine == "vector":
                nc.vector.tensor_copy(out=dst, in_=src)
            else:
                nc.scalar.copy(out=dst, in_=src)

        def round_plain(engine, grouped, raw, c0, c1):
            dst = grouped[:, c0 * PACK : c1 * PACK].rearrange("p (c w i) -> p c i w", w=RUN, i=PACK)
            copy_on(engine, dst, raw[:, :, c0:c1].rearrange("p i (c w) -> p c i w", w=RUN))

        def round_dealt(engine, grouped, raw, m0, m1, raw_m0=0):
            dst = grouped[:].rearrange("p (r m i) -> p m r i", r=PACK, i=PACK)[:, m0:m1, :, :]
            src = raw[:, :, (m0 - raw_m0) * PACK : (m1 - raw_m0) * PACK]
            copy_on(engine, dst, src.rearrange("p i (m r) -> p m r i", r=PACK))

        def shared_plain(grouped, raw):
            round_plain("vector", grouped, raw, 0, PLAIN_SPLIT)
            round_plain("scalar", grouped, raw, PLAIN_SPLIT, HALF)

        def shared_dealt(grouped, raw, m0, m1, split, raw_m0=0):
            round_dealt("vector", grouped, raw, m0, split, raw_m0)
            round_dealt("scalar", grouped, raw, split, m1, raw_m0)

        def load_gate(a):
            raw = sb.tile([P, PACK, M], F32, name="g%d_raw" % a, align_bytes=64)
            rows = g[half(a), :].rearrange("(p r) n -> p r n", r=PACK)
            for r0 in (0, 2):
                nc.sync.dma_start(out=raw[:, r0 : r0 + 2, :], in_=rows[:, r0 : r0 + 2, :])
            return raw

        def quantize(grouped, codes, scales):
            nc.vector.quantize_mx(out=codes.bitcast(FP8X4), scales=scales, in_=grouped)

        def quantize_operand(op):
            quantize(op[0][:], op[1][:], op[2][:])

        def scores(first_bank, keys, queries):
            banks = []
            for c in range(HALF // CHUNK):
                bank = ps.tile([P, PACK, CHUNK], F32, name="bank%d" % (first_bank + c))
                cols = slice(c * CHUNK, (c + 1) * CHUNK)
                for i in range(PACK):
                    rows = slice(i * P, (i + 1) * P)
                    nc.tensor.matmul_mx(
                        out=bank[:, i, :],
                        lhsT=keys[1][:, rows].bitcast(FP8X4),
                        lhsT_scale=keys[2][:, rows],
                        rhs=queries[1][:, cols].bitcast(FP8X4),
                        rhs_scale=queries[2][:, cols],
                        start=True,
                        stop=True,
                    )
                banks.append(bank)
            return banks

        def decay(h, banks, dm_block, c):
            m_cols = CHUNK // PACK
            dst = h[0][:].rearrange("p (r m i) -> p m r i", r=PACK, i=PACK)[:, c * m_cols : (c + 1) * m_cols, :, :]
            nc.vector.tensor_tensor(
                out=dst,
                in0=banks[c][:].rearrange("p i (m r) -> p m r i", r=PACK),
                in1=dm_block[:, :, c * CHUNK : (c + 1) * CHUNK].rearrange("p i (m r) -> p m r i", r=PACK),
                op=MULT,
            )

        def y_pass(banks, stationary, moving_codes, moving_scales, start, stop):
            for r in range(PACK):
                cols = slice(r * P, (r + 1) * P)
                nc.tensor.matmul_mx(
                    out=banks[r][:],
                    lhsT=stationary[1][:, cols].bitcast(FP8X4),
                    lhsT_scale=stationary[2][:, cols],
                    rhs=moving_codes,
                    rhs_scale=moving_scales,
                    start=start,
                    stop=stop,
                )

        def y_banks(first_bank):
            banks = []
            for r in range(PACK):
                bank = ps.tile([P, M], F32, name="bank%d" % (first_bank + r))
                banks.append(bank)
            return banks

        def gate(result, banks, g_raw, r):
            nc.vector.tensor_tensor(out=result[:, r, :], in0=banks[r][:], in1=g_raw[:, r, :], op=MULT)

        def store_rows(result, a, r0, r1):
            rows = out_0[half(a), :].rearrange("(p r) n -> p r n", r=PACK)
            nc.sync.dma_start(out=rows[:, r0:r1, :], in_=result[:, r0:r1, :])

        vc_plane = sb.tile([P, 2, M], U8, name="vc_plane", align_bytes=64)
        nc.vector.memset(vc_plane[:].rearrange("p a n -> p (a n)").bitcast(U32), 0)
        for q in range(QUADS):
            nc.scalar.dma_start(
                out=vc_plane[32 * q : 32 * q + 4, :, :].bitcast(I32),
                in_=vc_scales[:, 4 * q : 4 * q + 4, :].rearrange("a q n -> q a n").bitcast(I32),
            )

        kc_raw = load("kc_raw", kc)
        qc_raw = load("qc_raw", qc)
        dm0_raw = load("dm0_raw", dm[half(0), :])
        st_raw = load("st_raw", st)
        qd0_raw = load("qd0_raw", qd[:, half(0)])
        vc_codes = sb.tile([P, 2, 2 * M], U8, name="vc_codes", align_bytes=64)
        nc.sync.dma_start(out=vc_codes[:].bitcast(I32), in_=vc_words.rearrange("a p b -> p a b").bitcast(I32))
        dm11 = load("dm11_raw", dm[half(1), half(1)])
        qd1_raw = load("qd1_raw", qd[:, half(1)])
        g0_raw = load_gate(0)
        g1_raw = load_gate(1)

        kc_op = [new_operand("kc%d" % a) for a in range(2)]
        qc_op = [new_operand("qc%d" % a) for a in range(2)]
        qd_op = [new_operand("qd%d" % a) for a in range(2)]
        st_op = new_operand("st")
        h00, h01, h11 = new_operand("h00"), new_operand("h01"), new_operand("h11")
        vc_op = [(vc_codes[:, a, :].bitcast(FP4X4), vc_plane[:, a, :]) for a in range(2)]
        result = [sb.tile([P, PACK, M], F32, name="result%d" % a, align_bytes=64) for a in range(2)]
        out_bf = [sb.tile([P, M * PACK], BF16, name="out_bf%d" % a, align_bytes=64) for a in range(2)]
        out_codes = [sb.tile([P, M], U32, name="out_codes%d" % a, align_bytes=64) for a in range(2)]
        out_plane = sb.tile([P, 2, M], U8, name="out_plane", align_bytes=64)

        def out_planes(a):
            quantize(out_bf[a][:], out_codes[a][:], out_plane[:, a, :])
            nc.sync.dma_start(out=out_1[a].rearrange("p n i -> p (n i)").bitcast(I32), in_=out_codes[a][:].bitcast(I32))

        dm00, dm01 = dm0_raw[:, :, half(0)], dm0_raw[:, :, half(1)]
        st_codes, st_scales = st_op[1][:].bitcast(FP8X4), st_op[2][:]
        round_dealt("vector", kc_op[0][0], kc_raw[:, :, half(0)], 0, P)
        round_dealt("scalar", kc_op[1][0], kc_raw[:, :, half(1)], 0, P)
        quantize_operand(kc_op[0])
        quantize_operand(kc_op[1])
        round_plain("vector", qc_op[0][0], qc_raw[:, :, half(0)], 0, HALF)
        round_plain("scalar", qc_op[1][0], qc_raw[:, :, half(1)], 0, HALF)
        quantize_operand(qc_op[0])
        s00 = scores(0, kc_op[0], qc_op[0])
        quantize_operand(qc_op[1])
        s01 = scores(4, kc_op[0], qc_op[1])
        round_plain("scalar", st_op[0], st_raw[:], 0, M)
        round_dealt("scalar", qd_op[0][0], qd0_raw[:], 0, P)
        for c in range(4):
            decay(h00, s00, dm00, c)
        s11 = scores(0, kc_op[1], qc_op[1])
        decay(h01, s01, dm01, 0)
        quantize_operand(h00)
        for c in range(1, 4):
            decay(h01, s01, dm01, c)
        y0 = y_banks(4)
        y_pass(y0, h00, vc_op[0][0], vc_op[0][1], True, False)
        quantize_operand(st_op)
        quantize_operand(h01)
        quantize_operand(qd_op[0])
        y_pass(y0, qd_op[0], st_codes, st_scales, False, True)
        for c in range(4):
            decay(h11, s11, dm11[:], c)
        y1 = y_banks(0)
        y_pass(y1, h01, vc_op[0][0], vc_op[0][1], True, False)
        shared_dealt(qd_op[1][0], qd1_raw[:], 0, P, 32)
        quantize_operand(h11)
        y_pass(y1, h11, vc_op[1][0], vc_op[1][1], False, False)
        gate(result[0], y0, g0_raw, 0)
        gate(result[0], y0, g0_raw, 1)
        store_rows(result[0], 0, 0, 2)
        quantize_operand(qd_op[1])
        y_pass(y1, qd_op[1], st_codes, st_scales, False, True)
        gate(result[0], y0, g0_raw, 2)
        gate(result[0], y0, g0_raw, 3)
        store_rows(result[0], 0, 2, 4)
        round_plain("scalar", out_bf[0], result[0][:], 96, M)
        gate(result[1], y1, g1_raw, 0)
        gate(result[1], y1, g1_raw, 1)
        store_rows(result[1], 1, 0, 2)
        gate(result[1], y1, g1_raw, 2)
        gate(result[1], y1, g1_raw, 3)
        store_rows(result[1], 1, 2, 4)
        round_plain("vector", out_bf[0], result[0][:], 0, 96)
        round_plain("scalar", out_bf[1], result[1][:], 288, M)
        round_plain("vector", out_bf[1], result[1][:], 0, 288)
        out_planes(0)
        out_planes(1)
        for q in range(QUADS):
            engine = nc.sync if q % 2 == 0 else nc.scalar
            engine.dma_start(
                out=out_2[:, 4 * q : 4 * q + 4, :].rearrange("a q n -> q a n").bitcast(I32),
                in_=out_plane[32 * q : 32 * q + 4, :, :].bitcast(I32),
            )
